import numpy as np
import ml_dtypes


def mxq(x, axis, fmt="e4m3"):
    dtype, down = {"e4m3": (ml_dtypes.float8_e4m3fn, 7), "e5m2": (ml_dtypes.float8_e5m2, 14)}[fmt]
    v = np.moveaxis(np.asarray(x, np.float32).astype(ml_dtypes.bfloat16).astype(np.float64), axis, -1)
    blocks = v.reshape(v.shape[:-1] + (-1, 32))
    amax = np.abs(blocks).max(-1, keepdims=True)
    byte = np.maximum(np.where(amax > 0, np.frexp(amax)[1] - 1 + 127, 0) - down, 1)
    scale = np.exp2(byte - 127.0)
    codes = (blocks / scale).astype(np.float32).astype(dtype).astype(np.float64)
    return np.moveaxis((codes * scale).reshape(v.shape), -1, axis)


WIDE = False


def mx_kscale(k):
    if not WIDE:
        return np.ones(k)
    levels = np.array([10, -10, 5, -5, 0])
    if k % 512:
        return np.exp2(np.random.permutation(np.resize(levels, k // 32))).repeat(32)
    a = np.empty((k // 512, 16))
    for p in range(k // 512):
        a[p, :8] = np.random.permutation(np.resize(levels, 8))
        for g in range(8):
            far = levels[np.abs(levels - a[p, g]) >= 10]
            a[p, g + 8] = far[np.random.randint(len(far))]
    return np.exp2(a.ravel()).repeat(32)


def f64(x):
    return np.asarray(x).astype(np.float64)


def striped(idx):
    return np.tile(idx.reshape(-1, 16).T, (8, 1)).astype(np.uint16)


def unstriped(offs):
    return offs[:16].T.reshape(-1).astype(np.int64)


E2M1 = np.array([0.0, 0.5, 1.0, 1.5, 2.0, 3.0, 4.0, 6.0, -0.0, -0.5, -1.0, -1.5, -2.0, -3.0, -4.0, -6.0])


def pack_weight(w, fmt):
    k, n = w.shape
    w = f64(np.asarray(w, np.float32).astype(ml_dtypes.bfloat16)).reshape(k // 32, 32, n)
    amax = np.abs(w).max(1)
    if fmt == "e4m3":
        byte = np.frexp(amax)[1] - 1 + 127 - 7
    else:
        mant, ex = np.frexp(amax / 6.0)
        byte = np.where(mant > 0.5, ex, ex - 1) + 127
    byte = np.clip(np.where(amax > 0, byte, 1), 1, 254)
    scaled = (w * np.exp2(127.0 - byte)[:, None, :]).reshape(k, n).astype(np.float32)
    by_word = np.ascontiguousarray(scaled.reshape(k // 512, 128, 4, n).transpose(0, 1, 3, 2))
    if fmt == "e4m3":
        words = by_word.astype(ml_dtypes.float8_e4m3fn).view(np.uint8)
    else:
        c = by_word.astype(ml_dtypes.float4_e2m1fn).view(np.uint8) & 0xF
        words = (c[..., 0::2] | (c[..., 1::2] << 4)).reshape(k // 512, 128, 2 * n)
    return np.ascontiguousarray(words), np.ascontiguousarray(byte.astype(np.uint8).reshape(k // 512, 16, n))


def unpack_weight(words, scales, fmt):
    g, _, n = scales.shape
    words = np.ascontiguousarray(words).reshape(g, 128, n, -1)
    if fmt == "e4m3":
        vals = words.view(ml_dtypes.float8_e4m3fn).astype(np.float64)
    else:
        nib = np.empty((g, 128, n, 4), np.uint8)
        nib[..., 0::2] = words & 0xF
        nib[..., 1::2] = words >> 4
        vals = E2M1[nib]
    vals = vals * np.repeat(np.exp2(scales.astype(np.float64) - 127.0), 8, axis=1)[..., None]
    return vals.transpose(0, 1, 3, 2).reshape(g * 512, n)


def gelu(v):
    return 0.5 * v * (1.0 + np.tanh(np.sqrt(2.0 / np.pi) * (v + 0.044715 * v**3)))


def striped8(idx):
    return np.concatenate([v.reshape(-1, 16).T for v in idx]).astype(np.uint16)


def unstriped8(offs):
    return np.stack([offs[16 * g:16 * g + 16].T.reshape(-1) for g in range(8)]).astype(np.int64)


def put_heads(h, wgs, idx8, t2):
    r = np.arange(h.shape[0])
    page = np.zeros((h.shape[0], t2))
    page[r[:, None], idx8[r % 512 // 64]] = wgs[r // 4 % 128] * h
    return page


K, H, N, T, S, T2, P = 512, 1024, 384, 4096, 1024, 2048, 1024


def setup_inputs():
    n = np.random.standard_normal
    s = mx_kscale(K)[:, None]
    u = mx_kscale(H)[:, None]
    tab_words, tab_scales = pack_weight(n((K, T)) * s, "e4m3")
    wp_words, wp_scales = pack_weight(n((K, H)) * 0.38 / np.sqrt(K) / s, "e2m1")
    wk_words, wk_scales = pack_weight(n((K, N)) * 0.5 / np.sqrt(K) / s, "e4m3")
    slots = np.stack([np.random.permutation(T2)[:S] for _ in range(8)])
    return {
        "tab_words": tab_words, "tab_scales": tab_scales,
        "offs": striped(np.random.permutation(T)[:S]),
        "offs2": striped8(slots),
        "offs3": striped(np.random.permutation(T2)[:P]),
        "w1": (n((K, H)) * 0.6 / np.sqrt(K) / s * u.T).astype(np.float32),
        "wp_words": wp_words, "wp_scales": wp_scales,
        "phase": np.random.uniform(-0.9, 0.9, H).astype(np.float32),
        "gain": (np.random.uniform(1.6, 2.8, H) * u[:, 0]).astype(np.float32),
        "wgs": np.repeat(np.random.uniform(0.5, 2.0, (8, S)), 16, axis=0).astype(np.float32),
        "terrain": (n((H, P)) * 0.6 * u).astype(np.float32),
        "wo": (n((H, N)) * 0.9 / np.sqrt(H) / u).astype(np.float32),
        "wk_words": wk_words, "wk_scales": wk_scales,
    }


def reference(tab_words, tab_scales, offs, offs2, offs3, w1, wp_words, wp_scales, phase, gain, wgs, terrain, wo, wk_words, wk_scales):
    v = unpack_weight(tab_words, tab_scales, "e4m3")[:, unstriped(offs)]
    wp = unpack_weight(wp_words, wp_scales, "e2m1")
    wk = unpack_weight(wk_words, wk_scales, "e4m3")
    level = mxq(f64(w1), 0, "e4m3").T @ v
    angle = (wp.T @ v) + f64(phase)[:, None]
    h = level + f64(gain)[:, None] * np.sin(angle)
    page = put_heads(h, f64(wgs), unstriped8(offs2), T2)
    x = page[:, unstriped(offs3)]
    z = mxq(x + f64(terrain), 0, "e4m3")
    bent = np.tanh(mxq(f64(wo), 0, "e4m3").T @ z)
    out = bent + (wk.T @ v)
    return out

@@ -1,0 +1,227 @@
+from contextlib import ExitStack
+
+import concourse.mybir as mybir
+
+K, H, N, T, S, T2, PL = 512, 1024, 384, 4096, 1024, 2048, 1024
+FLOPS = 2 * (2 * K * H * S + H * N * PL + K * N * S)
+
+F32 = mybir.dt.float32
+BF16 = mybir.dt.bfloat16
+I32 = mybir.dt.int32
+U32 = mybir.dt.uint32
+U16 = mybir.dt.uint16
+U8 = mybir.dt.uint8
+FP8X4 = mybir.dt.float8_e4m3fn_x4
+FP4X4 = mybir.dt.float4_e2m1fn_x4
+ALU = mybir.AluOpType
+ACT = mybir.ActivationFunctionType
+
+P = 128
+PACK = 4
+BANK = 512
+BLOCKS = H // (P * PACK)
+NT = N // P
+CHUNK = 256
+
+
+def load_scale_rows(queue, plane, rows):
+    for q in range(4):
+        queue.dma_start(out=plane[32 * q : 32 * q + 4, :].bitcast(I32), in_=rows[4 * q : 4 * q + 4, :].bitcast(I32))
+
+
+def tile_list_sounding_path_features_kernel(
+    tc, tab_words, tab_scales, offs, offs2, offs3, w1, wp_words, wp_scales, phase, gain, wgs, terrain, wo, wk_words, wk_scales, out
+):
+    nc = tc.nc
+    with ExitStack() as ctx:
+        keep = ctx.enter_context(tc.tile_pool(name="keep", bufs=1))
+        ring = ctx.enter_context(tc.tile_pool(name="ring", bufs=2))
+        psum = ctx.enter_context(tc.psum_pool(name="psum", bufs=2))
+
+        list1 = keep.tile([P, S // 16], U16, name="list1")
+        list2 = keep.tile([P, S // 16], U16, name="list2")
+        list3 = keep.tile([P, PL // 16], U16, name="list3")
+        tab_w = keep.tile([P, T], I32, name="tab_w", align_bytes=64)
+        tab_s = keep.tile([P, T], U8, name="tab_s", align_bytes=64)
+        v_w = keep.tile([P, S], U32, name="v_w", align_bytes=64)
+        v_s = keep.tile([P, S], U8, name="v_s", align_bytes=64)
+        wp_raw_w = keep.tile([P, 2 * H], U8, name="wp_raw_w", align_bytes=64)
+        wp_raw_s = keep.tile([P, H], U8, name="wp_raw_s", align_bytes=64)
+        wp_w = keep.tile([P, 2 * H], U8, name="wp_w", align_bytes=64)
+        wp_s = keep.tile([P, H], U8, name="wp_s", align_bytes=64)
+        wk_w = keep.tile([P, N], I32, name="wk_w", align_bytes=64)
+        wk_s = keep.tile([P, N], U8, name="wk_s", align_bytes=64)
+        w1_raw = [keep.tile([P, PACK, BANK], F32, name="w1_raw%d" % b) for b in range(BLOCKS)]
+        w1_w = keep.tile([P, H], U32, name="w1_w", align_bytes=64)
+        w1_s = keep.tile([P, H], U8, name="w1_s", align_bytes=64)
+        wo_raw = [keep.tile([P, PACK, N], F32, name="wo_raw%d" % b) for b in range(BLOCKS)]
+        wo_w = keep.tile([P, BLOCKS * N], U32, name="wo_w", align_bytes=64)
+        wo_s = keep.tile([P, BLOCKS * N], U8, name="wo_s", align_bytes=64)
+        phase_sb = keep.tile([P, BLOCKS, PACK], F32, name="phase_sb")
+        gain_sb = keep.tile([P, BLOCKS, PACK], F32, name="gain_sb")
+        wgs_sb = keep.tile([P, S], F32, name="wgs_sb")
+        terr = [keep.tile([P, 2, PL], F32, name="terr%d" % u) for u in range(2 * BLOCKS)]
+        pages = [keep.tile([P, T2], F32, name="page%d" % u) for u in range(2)]
+        picked = [keep.tile([P, PACK, PL], F32, name="picked%d" % b) for b in range(BLOCKS)]
+        z_w = keep.tile([P, BLOCKS * PL], U32, name="z_w", align_bytes=64)
+        z_s = keep.tile([P, BLOCKS * PL], U8, name="z_s", align_bytes=64)
+        skip = keep.tile([P, NT, PL], F32, name="skip")
+
+        nc.vector.memset(wp_raw_s[:].bitcast(I32), 0)
+        nc.vector.memset(tab_s[:].bitcast(I32), 0)
+        nc.vector.memset(wk_s[:].bitcast(I32), 0)
+        for page in pages:
+            nc.vector.memset(page[:], 0.0)
+
+        nc.sync.dma_start(list1[:], offs)
+        nc.sync.dma_start(out=wp_raw_w[:].bitcast(I32), in_=wp_words[0].bitcast(I32))
+        load_scale_rows(nc.scalar, wp_raw_s, wp_scales[0])
+        nc.sync.dma_start(out=tab_w[:], in_=tab_words[0].rearrange("p t i -> p (t i)").bitcast(I32))
+        load_scale_rows(nc.sync, tab_s, tab_scales[0])
+        w1_rows = w1.rearrange("(p j) c -> p j c", j=PACK)
+        nc.sync.dma_start(out=w1_raw[0][:], in_=w1_rows[:, :, 0:BANK])
+        nc.scalar.dma_start(out=phase_sb[:], in_=phase.rearrange("(b p i) -> p b i", b=BLOCKS, i=PACK))
+        nc.scalar.dma_start(out=gain_sb[:], in_=gain.rearrange("(b p i) -> p b i", b=BLOCKS, i=PACK))
+        nc.sync.dma_start(out=wgs_sb[:], in_=wgs)
+        nc.sync.dma_start(list2[:], offs2)
+        nc.sync.dma_start(list3[:], offs3)
+        terr_rows = terrain.rearrange("(b p u e) j -> b u p e j", b=BLOCKS, u=2, e=2)
+        nc.sync.dma_start(out=terr[0][:], in_=terr_rows[0, 0])
+        nc.sync.dma_start(out=w1_raw[1][:], in_=w1_rows[:, :, BANK : 2 * BANK])
+        nc.sync.dma_start(out=terr[1][:], in_=terr_rows[0, 1])
+        nc.sync.dma_start(out=wk_w[:], in_=wk_words[0].rearrange("p c i -> p (c i)").bitcast(I32))
+        load_scale_rows(nc.sync, wk_s, wk_scales[0])
+        wo_rows = wo.rearrange("(b p i) n -> b p i n", b=BLOCKS, i=PACK)
+        for b in range(BLOCKS):
+            nc.sync.dma_start(out=wo_raw[b][:], in_=wo_rows[b])
+        for u in range(2):
+            nc.sync.dma_start(out=terr[2 + u][:], in_=terr_rows[1, u])
+
+        nc.vector.tensor_copy(
+            out=wp_s[:].rearrange("p (b i m) -> p b i m", b=BLOCKS, i=PACK),
+            in_=wp_raw_s[:].rearrange("p (b m i) -> p b i m", b=BLOCKS, i=PACK),
+        )
+        nc.vector.tensor_copy(
+            out=wp_w[:].rearrange("p (b i m e) -> p b i m e", b=BLOCKS, i=PACK, e=2),
+            in_=wp_raw_w[:].rearrange("p (b m i e) -> p b i m e", b=BLOCKS, i=PACK, e=2),
+        )
+
+        def entries(lst, first, count):
+            return lst[:, first // 16 : (first + count) // 16]
+
+        for c in range(0, S, BANK):
+            nc.vector.tensor_copy(v_w[:, c : c + BANK], tab_w[:].bitcast(U32).indirect(entries(list1, c, BANK)))
+        for c in range(0, S, BANK):
+            nc.vector.tensor_copy(v_s[:, c : c + BANK], tab_s[:].indirect(entries(list1, c, BANK)))
+
+        def quantise_w1(b, i0, i1):
+            grouped = ring.tile([P, PACK * BANK], BF16, name="w1_grouped", tag="grouped", align_bytes=64)
+            width = (i1 - i0) * BANK
+            nc.scalar.copy(
+                out=grouped[:, 0:width].rearrange("p (i m j) -> p m i j", j=PACK, m=P),
+                in_=w1_raw[b][:].rearrange("p j (m i) -> p m i j", i=PACK)[:, :, i0:i1, :],
+            )
+            cols = slice((PACK * b + i0) * P, (PACK * b + i1) * P)
+            nc.vector.quantize_mx(out=w1_w[:, cols].bitcast(FP8X4), scales=w1_s[:, cols], in_=grouped[:, 0:width])
+
+        def quantise_wo(b):
+            grouped = ring.tile([P, PACK * BANK], BF16, name="wo_grouped", tag="grouped", align_bytes=64)
+            nc.scalar.copy(
+                out=grouped[:, 0 : PACK * N].rearrange("p (c e i) -> p c i e", e=4, i=PACK),
+                in_=wo_raw[b][:].rearrange("p i (c e) -> p c i e", e=4),
+            )
+            cols = slice(b * N, (b + 1) * N)
+            nc.vector.quantize_mx(out=wo_w[:, cols].bitcast(FP8X4), scales=wo_s[:, cols], in_=grouped[:, 0 : PACK * N])
+
+        def quantise_z(b, c, width):
+            grouped = ring.tile([P, PACK * BANK], BF16, name="z_grouped", tag="grouped", align_bytes=64)
+            nc.scalar.copy(
+                out=grouped[:, 0 : PACK * width].rearrange("p (c e i) -> p c i e", e=4, i=PACK),
+                in_=picked[b][:, :, c : c + width].rearrange("p i (c e) -> p c i e", e=4),
+            )
+            cols = slice(b * PL + c, b * PL + c + width)
+            nc.vector.quantize_mx(out=z_w[:, cols].bitcast(FP8X4), scales=z_s[:, cols], in_=grouped[:, 0 : PACK * width])
+
+        def with_table(acc, w_codes, w_scales, c):
+            nc.tensor.matmul_mx(
+                out=acc, lhsT=w_codes, lhsT_scale=w_scales,
+                rhs=v_w[:, c : c + BANK].bitcast(FP8X4), rhs_scale=v_s[:, c : c + BANK], start=True, stop=True,
+            )
+
+        def features(b, i):
+            t = PACK * b + i
+            cols = slice(t * P, (t + 1) * P)
+            h = ring.tile([P, S], F32, name="h")
+            for c in range(0, S, BANK):
+                angle = psum.tile([P, BANK], F32, name="angle")
+                with_table(angle[:], wp_w[:, 2 * t * P : 2 * (t + 1) * P].bitcast(FP4X4), wp_s[:, cols], c)
+                level = psum.tile([P, BANK], F32, name="level")
+                with_table(level[:], w1_w[:, cols].bitcast(FP8X4), w1_s[:, cols], c)
+                sine = ring.tile([P, BANK], F32, name="sine")
+                nc.scalar.activation(out=sine[:], in_=angle[:], func=ACT.Sin, bias=phase_sb[:, b, i : i + 1])
+                nc.vector.scalar_tensor_tensor(
+                    out=h[:, c : c + BANK], in0=sine[:], scalar=gain_sb[:, b, i : i + 1], in1=level[:], op0=ALU.mult, op1=ALU.add
+                )
+            return h
+
+        def put(t, h):
+            nc.vector.tensor_tensor(pages[t % 2][:].indirect(list2[:]), h[:], wgs_sb[:], ALU.mult)
+
+        def fetch(b, i, c, width):
+            t = PACK * b + i
+            nc.vector.tensor_tensor(
+                picked[b][:, i, c : c + width], pages[t % 2][:].indirect(entries(list3, c, width)),
+                terr[t // 2][:, t % 2, c : c + width], ALU.add,
+            )
+
+        def skip_product(n, c):
+            acc = psum.tile([P, BANK], F32, name="second")
+            cols = slice(n * P, (n + 1) * P)
+            with_table(acc[:], wk_w[:, cols].bitcast(FP8X4), wk_s[:, cols], c)
+            nc.scalar.copy(out=skip[:, n, c : c + BANK], in_=acc[:])
+
+        quantise_w1(0, 0, 1)
+        for b in range(BLOCKS):
+            for i in range(PACK):
+                t = PACK * b + i
+                h = features(b, i)
+                put(t, h)
+                if t == 0:
+                    quantise_w1(0, 1, PACK)
+                if t == 1:
+                    quantise_w1(1, 0, PACK)
+                if t < PACK * BLOCKS - 1:
+                    fetch(b, i, 0, PL)
+                if t == 2:
+                    for n in range(NT):
+                        for c in range(0, S, BANK):
+                            skip_product(n, c)
+                if t in (3, 4):
+                    quantise_wo(t - 3)
+                if t in (5, 6):
+                    quantise_z(0, (t - 5) * BANK, BANK)
+
+        out_rows = out.rearrange("(n p) j -> p n j", p=P)
+        for c in range(0, PL, CHUNK):
+            fetch(BLOCKS - 1, PACK - 1, c, CHUNK)
+        for c in range(0, PL, CHUNK):
+            quantise_z(BLOCKS - 1, c, CHUNK)
+            bent = ring.tile([P, NT, CHUNK], F32, name="bent")
+            for n0, n1 in ((0, 2), (2, 3)):
+                acc = psum.tile([P, BANK], F32, name="second")
+                for n in range(n0, n1):
+                    for b in range(BLOCKS):
+                        w_cols = slice(b * N + n * P, b * N + (n + 1) * P)
+                        z_cols = slice(b * PL + c, b * PL + c + CHUNK)
+                        nc.tensor.matmul_mx(
+                            out=acc[:, (n - n0) * CHUNK : (n - n0 + 1) * CHUNK],
+                            lhsT=wo_w[:, w_cols].bitcast(FP8X4), lhsT_scale=wo_s[:, w_cols],
+                            rhs=z_w[:, z_cols].bitcast(FP8X4), rhs_scale=z_s[:, z_cols],
+                            start=(b == 0), stop=(b == BLOCKS - 1),
+                        )
+                nc.scalar.activation(
+                    out=bent[:, n0:n1, :].rearrange("p n j -> p (n j)"), in_=acc[:, 0 : (n1 - n0) * CHUNK], func=ACT.Tanh
+                )
+            result = ring.tile([P, NT, CHUNK], F32, name="result")
+            nc.vector.tensor_tensor(result[:], bent[:], skip[:, :, c : c + CHUNK], ALU.add)
+            nc.sync.dma_start(out=out_rows[:, :, c : c + CHUNK], in_=result[:])

@@ -1,6 +1,7 @@
 from contextlib import ExitStack
 
 import concourse.mybir as mybir
+from concourse.masks import make_identity
 
 K, H, N, T, S, T2, PL = 512, 1024, 384, 4096, 1024, 2048, 1024
 FLOPS = 2 * (2 * K * H * S + H * N * PL + K * N * S)
@@ -21,12 +22,12 @@ PACK = 4
 BANK = 512
 BLOCKS = H // (P * PACK)
 NT = N // P
-CHUNK = 256
+CHUNKS = (256, 256, 256, 128, 128)
 
 
-def load_scale_rows(queue, plane, rows):
-    for q in range(4):
-        queue.dma_start(out=plane[32 * q : 32 * q + 4, :].bitcast(I32), in_=rows[4 * q : 4 * q + 4, :].bitcast(I32))
+def load_scale_rows(queue, plane, rows, places):
+    for r in places:
+        queue.dma_start(out=plane[r:P:32, :].bitcast(I32), in_=rows[r:16:4, :].bitcast(I32))
 
 
 def tile_list_sounding_path_features_kernel(
@@ -35,8 +36,18 @@ def tile_list_sounding_path_features_kernel(
     nc = tc.nc
     with ExitStack() as ctx:
         keep = ctx.enter_context(tc.tile_pool(name="keep", bufs=1))
-        ring = ctx.enter_context(tc.tile_pool(name="ring", bufs=2))
-        psum = ctx.enter_context(tc.psum_pool(name="psum", bufs=2))
+        psum = ctx.enter_context(tc.psum_pool(name="psum", bufs=1))
+
+        def several(name, count, shape, dtype):
+            return [keep.tile(shape, dtype, name="%s%d" % (name, u), align_bytes=64) for u in range(count)]
+
+        banks = [psum.tile([P, BANK], F32, name="bank%d" % u) for u in range(8)]
+        angle_banks, level_banks, turned_banks, back_banks = banks[0:2], banks[2:4], banks[4:6], banks[6:8]
+        grouped_tiles = several("grouped", 2, [P, PACK * BANK], BF16)
+        h_tiles = several("h", 3, [P, S], F32)
+        sine_tiles = several("sine", 2, [P, BANK], F32)
+        level_tiles = several("level_sb", 2, [P, BANK], F32)
+        turned_tiles = several("turned_sb", 2, [P, BANK], F32)
 
         list1 = keep.tile([P, S // 16], U16, name="list1")
         list2 = keep.tile([P, S // 16], U16, name="list2")
@@ -44,56 +55,67 @@ def tile_list_sounding_path_features_kernel(
         tab_w = keep.tile([P, T], I32, name="tab_w", align_bytes=64)
         tab_s = keep.tile([P, T], U8, name="tab_s", align_bytes=64)
         v_w = keep.tile([P, S], U32, name="v_w", align_bytes=64)
-        v_s = keep.tile([P, S], U8, name="v_s", align_bytes=64)
+        shared = ctx.enter_context(tc.tile_pool(name="shared", bufs=1))
+        first_grouped = shared.tile([P, 2 * BANK], BF16, name="first_grouped", align_bytes=64, offset=0)
+        first_sine = shared.tile([P, BANK], F32, name="first_sine", align_bytes=64, offset=BANK)
+        v_s = [
+            keep.tile([P, BANK], U8, name="v_s0", align_bytes=64),
+            shared.tile([P, BANK], U8, name="v_s1", align_bytes=64, offset=0),
+        ]
         wp_raw_w = keep.tile([P, 2 * H], U8, name="wp_raw_w", align_bytes=64)
         wp_raw_s = keep.tile([P, H], U8, name="wp_raw_s", align_bytes=64)
         wp_w = keep.tile([P, 2 * H], U8, name="wp_w", align_bytes=64)
         wp_s = keep.tile([P, H], U8, name="wp_s", align_bytes=64)
         wk_w = keep.tile([P, N], I32, name="wk_w", align_bytes=64)
         wk_s = keep.tile([P, N], U8, name="wk_s", align_bytes=64)
-        w1_raw = [keep.tile([P, PACK, BANK], F32, name="w1_raw%d" % b) for b in range(BLOCKS)]
+        w1_raw = several("w1_raw", 2 * BLOCKS, [P, PACK, BANK // 2], F32)
         w1_w = keep.tile([P, H], U32, name="w1_w", align_bytes=64)
         w1_s = keep.tile([P, H], U8, name="w1_s", align_bytes=64)
-        wo_raw = [keep.tile([P, PACK, N], F32, name="wo_raw%d" % b) for b in range(BLOCKS)]
+        wo_raw = keep.tile([P, PACK, N], F32, name="wo_raw")
+        ident = keep.tile([P, P], F32, name="ident")
+        z_first = [keep.tile([P, PACK * BANK], BF16, name="z_first%d" % u, align_bytes=64) for u in range(2)]
+        z_last = keep.tile([P, PACK * PL], BF16, name="z_last", align_bytes=64)
         wo_w = keep.tile([P, BLOCKS * N], U32, name="wo_w", align_bytes=64)
         wo_s = keep.tile([P, BLOCKS * N], U8, name="wo_s", align_bytes=64)
         phase_sb = keep.tile([P, BLOCKS, PACK], F32, name="phase_sb")
         gain_sb = keep.tile([P, BLOCKS, PACK], F32, name="gain_sb")
         wgs_sb = keep.tile([P, S], F32, name="wgs_sb")
         terr = [keep.tile([P, 2, PL], F32, name="terr%d" % u) for u in range(2 * BLOCKS)]
-        pages = [keep.tile([P, T2], F32, name="page%d" % u) for u in range(2)]
+        pages = [keep.tile([P, T2], F32, name="page%d" % u) for u in range(3)]
         picked = [keep.tile([P, PACK, PL], F32, name="picked%d" % b) for b in range(BLOCKS)]
         z_w = keep.tile([P, BLOCKS * PL], U32, name="z_w", align_bytes=64)
         z_s = keep.tile([P, BLOCKS * PL], U8, name="z_s", align_bytes=64)
         skip = keep.tile([P, NT, PL], F32, name="skip")
 
-        nc.vector.memset(wp_raw_s[:].bitcast(I32), 0)
-        nc.vector.memset(tab_s[:].bitcast(I32), 0)
-        nc.vector.memset(wk_s[:].bitcast(I32), 0)
-        for page in pages:
-            nc.vector.memset(page[:], 0.0)
+        nc.gpsimd.memset(wp_raw_s[:].bitcast(I32), 0)
+        nc.gpsimd.memset(tab_s[:].bitcast(I32), 0)
+        nc.gpsimd.memset(wk_s[:].bitcast(I32), 0)
+        make_identity(nc, ident[:])
+        for page, engine in zip(pages, (nc.vector, nc.vector, nc.gpsimd)):
+            engine.memset(page[:], 0.0)
 
         nc.sync.dma_start(list1[:], offs)
-        nc.sync.dma_start(out=wp_raw_w[:].bitcast(I32), in_=wp_words[0].bitcast(I32))
-        load_scale_rows(nc.scalar, wp_raw_s, wp_scales[0])
+        load_scale_rows(nc.sync, wp_raw_s, wp_scales[0], range(0, 3))
         nc.sync.dma_start(out=tab_w[:], in_=tab_words[0].rearrange("p t i -> p (t i)").bitcast(I32))
-        load_scale_rows(nc.sync, tab_s, tab_scales[0])
-        w1_rows = w1.rearrange("(p j) c -> p j c", j=PACK)
-        nc.sync.dma_start(out=w1_raw[0][:], in_=w1_rows[:, :, 0:BANK])
-        nc.scalar.dma_start(out=phase_sb[:], in_=phase.rearrange("(b p i) -> p b i", b=BLOCKS, i=PACK))
-        nc.scalar.dma_start(out=gain_sb[:], in_=gain.rearrange("(b p i) -> p b i", b=BLOCKS, i=PACK))
+        load_scale_rows(nc.sync, wp_raw_s, wp_scales[0], range(3, 4))
+        load_scale_rows(nc.sync, tab_s, tab_scales[0], range(4))
+        nc.sync.dma_start(out=wp_raw_w[:].bitcast(I32), in_=wp_words[0].bitcast(I32))
+        w1_rows = w1.rearrange("(p j) (u c) -> u p j c", j=PACK, u=2 * BLOCKS)
+        for u in range(2):
+            nc.sync.dma_start(out=w1_raw[u][:], in_=w1_rows[u])
+        nc.sync.dma_start(out=phase_sb[:], in_=phase.rearrange("(b p i) -> p b i", b=BLOCKS, i=PACK))
+        nc.sync.dma_start(out=gain_sb[:], in_=gain.rearrange("(b p i) -> p b i", b=BLOCKS, i=PACK))
         nc.sync.dma_start(out=wgs_sb[:], in_=wgs)
         nc.sync.dma_start(list2[:], offs2)
         nc.sync.dma_start(list3[:], offs3)
         terr_rows = terrain.rearrange("(b p u e) j -> b u p e j", b=BLOCKS, u=2, e=2)
         nc.sync.dma_start(out=terr[0][:], in_=terr_rows[0, 0])
-        nc.sync.dma_start(out=w1_raw[1][:], in_=w1_rows[:, :, BANK : 2 * BANK])
+        for u in range(2, 4):
+            nc.sync.dma_start(out=w1_raw[u][:], in_=w1_rows[u])
         nc.sync.dma_start(out=terr[1][:], in_=terr_rows[0, 1])
         nc.sync.dma_start(out=wk_w[:], in_=wk_words[0].rearrange("p c i -> p (c i)").bitcast(I32))
-        load_scale_rows(nc.sync, wk_s, wk_scales[0])
+        load_scale_rows(nc.sync, wk_s, wk_scales[0], range(4))
         wo_rows = wo.rearrange("(b p i) n -> b p i n", b=BLOCKS, i=PACK)
-        for b in range(BLOCKS):
-            nc.sync.dma_start(out=wo_raw[b][:], in_=wo_rows[b])
         for u in range(2):
             nc.sync.dma_start(out=terr[2 + u][:], in_=terr_rows[1, u])
 
@@ -101,9 +123,9 @@ def tile_list_sounding_path_features_kernel(
             out=wp_s[:].rearrange("p (b i m) -> p b i m", b=BLOCKS, i=PACK),
             in_=wp_raw_s[:].rearrange("p (b m i) -> p b i m", b=BLOCKS, i=PACK),
         )
-        nc.vector.tensor_copy(
-            out=wp_w[:].rearrange("p (b i m e) -> p b i m e", b=BLOCKS, i=PACK, e=2),
-            in_=wp_raw_w[:].rearrange("p (b m i e) -> p b i m e", b=BLOCKS, i=PACK, e=2),
+        nc.scalar.copy(
+            out=wp_w[:].bitcast(U16).rearrange("p (b i m) -> p b m i", b=BLOCKS, i=PACK),
+            in_=wp_raw_w[:].bitcast(U16).rearrange("p (b m i) -> p b m i", b=BLOCKS, i=PACK),
         )
 
         def entries(lst, first, count):
@@ -111,117 +133,171 @@ def tile_list_sounding_path_features_kernel(
 
         for c in range(0, S, BANK):
             nc.vector.tensor_copy(v_w[:, c : c + BANK], tab_w[:].bitcast(U32).indirect(entries(list1, c, BANK)))
-        for c in range(0, S, BANK):
-            nc.vector.tensor_copy(v_s[:, c : c + BANK], tab_s[:].indirect(entries(list1, c, BANK)))
 
-        def quantise_w1(b, i0, i1):
-            grouped = ring.tile([P, PACK * BANK], BF16, name="w1_grouped", tag="grouped", align_bytes=64)
+        def gather_scales(u):
+            nc.vector.tensor_copy(v_s[u][:], tab_s[:].indirect(entries(list1, u * BANK, BANK)))
+
+        def quantise_w1(grouped, b, i0, i1):
             width = (i1 - i0) * BANK
-            nc.scalar.copy(
-                out=grouped[:, 0:width].rearrange("p (i m j) -> p m i j", j=PACK, m=P),
-                in_=w1_raw[b][:].rearrange("p j (m i) -> p m i j", i=PACK)[:, :, i0:i1, :],
-            )
+            for u in range(2):
+                nc.scalar.copy(
+                    out=grouped[:, 0:width].rearrange("p (i m j) -> p m i j", j=PACK, m=P)[:, u * P // 2 : (u + 1) * P // 2],
+                    in_=w1_raw[2 * b + u][:].rearrange("p j (m i) -> p m i j", i=PACK)[:, :, i0:i1, :],
+                )
             cols = slice((PACK * b + i0) * P, (PACK * b + i1) * P)
             nc.vector.quantize_mx(out=w1_w[:, cols].bitcast(FP8X4), scales=w1_s[:, cols], in_=grouped[:, 0:width])
 
         def quantise_wo(b):
-            grouped = ring.tile([P, PACK * BANK], BF16, name="wo_grouped", tag="grouped", align_bytes=64)
+            nc.sync.dma_start(out=wo_raw[:], in_=wo_rows[b])
+            grouped = grouped_tiles[b]
             nc.scalar.copy(
                 out=grouped[:, 0 : PACK * N].rearrange("p (c e i) -> p c i e", e=4, i=PACK),
-                in_=wo_raw[b][:].rearrange("p i (c e) -> p c i e", e=4),
+                in_=wo_raw[:].rearrange("p i (c e) -> p c i e", e=4),
             )
             cols = slice(b * N, (b + 1) * N)
             nc.vector.quantize_mx(out=wo_w[:, cols].bitcast(FP8X4), scales=wo_s[:, cols], in_=grouped[:, 0 : PACK * N])
 
-        def quantise_z(b, c, width):
-            grouped = ring.tile([P, PACK * BANK], BF16, name="z_grouped", tag="grouped", align_bytes=64)
-            nc.scalar.copy(
-                out=grouped[:, 0 : PACK * width].rearrange("p (c e i) -> p c i e", e=4, i=PACK),
-                in_=picked[b][:, :, c : c + width].rearrange("p i (c e) -> p c i e", e=4),
+        def weave(copy, grouped, b, i0, i1, c, width):
+            copy(
+                out=grouped.rearrange("p (c e i) -> p c i e", e=4, i=PACK)[:, :, i0:i1, :],
+                in_=picked[b][:, i0:i1, c : c + width].rearrange("p i (c e) -> p c i e", e=4),
             )
+
+        def quantise_z(grouped, b, c, width):
             cols = slice(b * PL + c, b * PL + c + width)
-            nc.vector.quantize_mx(out=z_w[:, cols].bitcast(FP8X4), scales=z_s[:, cols], in_=grouped[:, 0 : PACK * width])
+            nc.vector.quantize_mx(out=z_w[:, cols].bitcast(FP8X4), scales=z_s[:, cols], in_=grouped)
 
         def with_table(acc, w_codes, w_scales, c):
             nc.tensor.matmul_mx(
                 out=acc, lhsT=w_codes, lhsT_scale=w_scales,
-                rhs=v_w[:, c : c + BANK].bitcast(FP8X4), rhs_scale=v_s[:, c : c + BANK], start=True, stop=True,
+                rhs=v_w[:, c : c + BANK].bitcast(FP8X4), rhs_scale=v_s[c // BANK][:], start=True, stop=True,
             )
 
-        def features(b, i):
+        def features(b, i, on_vector):
             t = PACK * b + i
             cols = slice(t * P, (t + 1) * P)
-            h = ring.tile([P, S], F32, name="h")
+            h = h_tiles[t % 3]
             for c in range(0, S, BANK):
-                angle = psum.tile([P, BANK], F32, name="angle")
+                u = c // BANK
+                angle = angle_banks[u]
                 with_table(angle[:], wp_w[:, 2 * t * P : 2 * (t + 1) * P].bitcast(FP4X4), wp_s[:, cols], c)
-                level = psum.tile([P, BANK], F32, name="level")
+                level = level_banks[u]
                 with_table(level[:], w1_w[:, cols].bitcast(FP8X4), w1_s[:, cols], c)
-                sine = ring.tile([P, BANK], F32, name="sine")
-                nc.scalar.activation(out=sine[:], in_=angle[:], func=ACT.Sin, bias=phase_sb[:, b, i : i + 1])
-                nc.vector.scalar_tensor_tensor(
-                    out=h[:, c : c + BANK], in0=sine[:], scalar=gain_sb[:, b, i : i + 1], in1=level[:], op0=ALU.mult, op1=ALU.add
-                )
+                sine = first_sine[:] if (t, u) == (0, 0) else sine_tiles[u][:]
+                nc.scalar.activation(out=sine, in_=angle[:], func=ACT.Sin, bias=phase_sb[:, b, i : i + 1])
+                if on_vector:
+                    nc.vector.scalar_tensor_tensor(
+                        out=h[:, c : c + BANK], in0=sine, scalar=gain_sb[:, b, i : i + 1], in1=level[:], op0=ALU.mult, op1=ALU.add
+                    )
+                    if t == 0:
+                        put(t, h, c, BANK)
+                    continue
+                level_sb = picked[1][:, 2, 0:BANK] if (t, u) == (7, 1) else level_tiles[u][:]
+                nc.scalar.copy(out=level_sb, in_=level[:])
+                nc.scalar.activation(out=sine, in_=sine, func=ACT.Copy, scale=gain_sb[:, b, i : i + 1])
+                turned = turned_banks[u]
+                for q in range(0, BANK, P):
+                    for term, first in ((level_sb, True), (sine, False)):
+                        nc.tensor.matmul(
+                            turned[:, q : q + P], lhsT=term[:, q : q + P], rhs=ident[:], is_transpose=True, start=first, stop=not first
+                        )
+                if c > 0 and t in late_tiles:
+                    turned_sb = late_tiles[t][:].bitcast(F32)[:, 0:BANK]
+                elif c == 0 and t >= 5:
+                    turned_sb = picked[(t - 2) // PACK][:, (t - 2) % PACK, 0:BANK]
+                else:
+                    turned_sb = turned_tiles[u][:]
+                nc.scalar.copy(out=turned_sb, in_=turned[:])
+                back = back_banks[u]
+                for q in range(0, BANK, P):
+                    nc.tensor.transpose(back[:, q : q + P], turned_sb[:, q : q + P], ident[:])
+                nc.scalar.copy(out=h[:, c : c + BANK], in_=back[:])
             return h
 
-        def put(t, h):
-            nc.vector.tensor_tensor(pages[t % 2][:].indirect(list2[:]), h[:], wgs_sb[:], ALU.mult)
+        def put(t, h, c, width):
+            nc.vector.tensor_tensor(
+                pages[t % 3][:].indirect(entries(list2, c, width)), h[:, c : c + width], wgs_sb[:, c : c + width], ALU.mult
+            )
 
         def fetch(b, i, c, width):
             t = PACK * b + i
             nc.vector.tensor_tensor(
-                picked[b][:, i, c : c + width], pages[t % 2][:].indirect(entries(list3, c, width)),
+                picked[b][:, i, c : c + width], pages[t % 3][:].indirect(entries(list3, c, width)),
                 terr[t // 2][:, t % 2, c : c + width], ALU.add,
             )
 
         def skip_product(n, c):
-            acc = psum.tile([P, BANK], F32, name="second")
+            acc = banks[(2 * n + c // BANK) % 4]
             cols = slice(n * P, (n + 1) * P)
             with_table(acc[:], wk_w[:, cols].bitcast(FP8X4), wk_s[:, cols], c)
             nc.scalar.copy(out=skip[:, n, c : c + BANK], in_=acc[:])
 
-        quantise_w1(0, 0, 1)
+        late_tiles = {5: z_first[0], 6: z_first[1], 7: z_last}
+        gather_scales(0)
+        quantise_w1(first_grouped, 0, 0, 2)
+        gather_scales(1)
         for b in range(BLOCKS):
             for i in range(PACK):
                 t = PACK * b + i
-                h = features(b, i)
-                put(t, h)
+                h = features(b, i, t < 2)
+                if t >= 5:
+                    fetch((t - 2) // PACK, (t - 2) % PACK, 0, PL)
+                if t == 7:
+                    fetch(1, 2, 0, PL)
+                if t > 0:
+                    put(t, h, 0, S)
                 if t == 0:
-                    quantise_w1(0, 1, PACK)
-                if t == 1:
-                    quantise_w1(1, 0, PACK)
-                if t < PACK * BLOCKS - 1:
-                    fetch(b, i, 0, PL)
+                    quantise_w1(grouped_tiles[1], 0, 2, PACK)
                 if t == 2:
-                    for n in range(NT):
-                        for c in range(0, S, BANK):
-                            skip_product(n, c)
-                if t in (3, 4):
-                    quantise_wo(t - 3)
+                    quantise_w1(z_first[1], 1, 0, PACK)
+                if t < 3:
+                    fetch(b, i, 0, PL)
+                if t in (4, 5):
+                    quantise_wo(t - 4)
                 if t in (5, 6):
-                    quantise_z(0, (t - 5) * BANK, BANK)
+                    weave(nc.scalar.copy, z_first[t - 5][:], 0, 0, PACK, (t - 5) * BANK, BANK)
+                    quantise_z(z_first[t - 5][:], 0, (t - 5) * BANK, BANK)
+        for n in range(NT):
+            for c in range(0, S, BANK):
+                skip_product(n, c)
+        weave(nc.scalar.copy, z_last[:], 1, 0, 2, 0, PL)
 
         out_rows = out.rearrange("(n p) j -> p n j", p=P)
-        for c in range(0, PL, CHUNK):
-            fetch(BLOCKS - 1, PACK - 1, c, CHUNK)
-        for c in range(0, PL, CHUNK):
-            quantise_z(BLOCKS - 1, c, CHUNK)
-            bent = ring.tile([P, NT, CHUNK], F32, name="bent")
-            for n0, n1 in ((0, 2), (2, 3)):
-                acc = psum.tile([P, BANK], F32, name="second")
+        chunks = []
+        free_banks = list(banks)
+        first = 0
+        for width in CHUNKS:
+            per_bank = BANK // width
+            sums = [(free_banks.pop(), n0, min(n0 + per_bank, NT)) for n0 in range(0, NT, per_bank)]
+            chunks.append((first, width, sums))
+            first = first + width
+
+        def second_stage(b, c, width, sums):
+            z_cols = slice(b * PL + c, b * PL + c + width)
+            for acc, n0, n1 in sums:
                 for n in range(n0, n1):
-                    for b in range(BLOCKS):
-                        w_cols = slice(b * N + n * P, b * N + (n + 1) * P)
-                        z_cols = slice(b * PL + c, b * PL + c + CHUNK)
-                        nc.tensor.matmul_mx(
-                            out=acc[:, (n - n0) * CHUNK : (n - n0 + 1) * CHUNK],
-                            lhsT=wo_w[:, w_cols].bitcast(FP8X4), lhsT_scale=wo_s[:, w_cols],
-                            rhs=z_w[:, z_cols].bitcast(FP8X4), rhs_scale=z_s[:, z_cols],
-                            start=(b == 0), stop=(b == BLOCKS - 1),
-                        )
-                nc.scalar.activation(
-                    out=bent[:, n0:n1, :].rearrange("p n j -> p (n j)"), in_=acc[:, 0 : (n1 - n0) * CHUNK], func=ACT.Tanh
-                )
-            result = ring.tile([P, NT, CHUNK], F32, name="result")
-            nc.vector.tensor_tensor(result[:], bent[:], skip[:, :, c : c + CHUNK], ALU.add)
-            nc.sync.dma_start(out=out_rows[:, :, c : c + CHUNK], in_=result[:])
+                    w_cols = slice(b * N + n * P, b * N + (n + 1) * P)
+                    nc.tensor.matmul_mx(
+                        out=acc[:, (n - n0) * width : (n - n0 + 1) * width],
+                        lhsT=wo_w[:, w_cols].bitcast(FP8X4), lhsT_scale=wo_s[:, w_cols],
+                        rhs=z_w[:, z_cols].bitcast(FP8X4), rhs_scale=z_s[:, z_cols],
+                        start=(b == 0 and n == n0), stop=(b == BLOCKS - 1 and n == n1 - 1),
+                    )
+
+        for c, width, sums in chunks:
+            second_stage(0, c, width, sums)
+        for c, width, sums in chunks:
+            fetch(BLOCKS - 1, PACK - 1, c, width)
+        for c, width, sums in chunks:
+            grouped = z_last[:, PACK * c : PACK * (c + width)]
+            weave(nc.scalar.copy, grouped, 1, 2, PACK, c, width)
+            quantise_z(grouped, 1, c, width)
+        for k, (c, width, sums) in enumerate(chunks):
+            second_stage(1, c, width, sums)
+            bent = h_tiles[k % 3]
+            for acc, n0, n1 in sums:
+                nc.scalar.activation(out=bent[:, n0 * width : n1 * width], in_=acc[:, 0 : (n1 - n0) * width], func=ACT.Tanh)
+            nc.vector.tensor_tensor(
+                skip[:, :, c : c + width], bent[:, 0 : NT * width].rearrange("p (n j) -> p n j", n=NT), skip[:, :, c : c + width], ALU.add
+            )
+            nc.sync.dma_start(out=out_rows[:, :, c : c + width], in_=skip[:, :, c : c + width])

@@ -73,7 +73,7 @@ def tile_list_sounding_path_features_kernel(
         w1_s = keep.tile([P, H], U8, name="w1_s", align_bytes=64)
         wo_raw = keep.tile([P, PACK, N], F32, name="wo_raw")
         ident = keep.tile([P, P], F32, name="ident")
-        z_first = [keep.tile([P, PACK * BANK], BF16, name="z_first%d" % u, align_bytes=64) for u in range(2)]
+        z_first = keep.tile([P, PACK * PL], BF16, name="z_first", align_bytes=64)
         z_last = keep.tile([P, PACK * PL], BF16, name="z_last", align_bytes=64)
         wo_w = keep.tile([P, BLOCKS * N], U32, name="wo_w", align_bytes=64)
         wo_s = keep.tile([P, BLOCKS * N], U8, name="wo_s", align_bytes=64)
@@ -91,8 +91,8 @@ def tile_list_sounding_path_features_kernel(
         nc.gpsimd.memset(tab_s[:].bitcast(I32), 0)
         nc.gpsimd.memset(wk_s[:].bitcast(I32), 0)
         make_identity(nc, ident[:])
-        for page, engine in zip(pages, (nc.vector, nc.vector, nc.gpsimd)):
-            engine.memset(page[:], 0.0)
+        for page in pages:
+            nc.vector.memset(page[:], 0.0)
 
         nc.sync.dma_start(list1[:], offs)
         load_scale_rows(nc.sync, wp_raw_s, wp_scales[0], range(0, 3))
@@ -109,12 +109,12 @@ def tile_list_sounding_path_features_kernel(
         nc.sync.dma_start(list2[:], offs2)
         nc.sync.dma_start(list3[:], offs3)
         terr_rows = terrain.rearrange("(b p u e) j -> b u p e j", b=BLOCKS, u=2, e=2)
-        nc.sync.dma_start(out=terr[0][:], in_=terr_rows[0, 0])
         for u in range(2, 4):
             nc.sync.dma_start(out=w1_raw[u][:], in_=w1_rows[u])
-        nc.sync.dma_start(out=terr[1][:], in_=terr_rows[0, 1])
+        nc.sync.dma_start(out=terr[0][:], in_=terr_rows[0, 0])
         nc.sync.dma_start(out=wk_w[:], in_=wk_words[0].rearrange("p c i -> p (c i)").bitcast(I32))
         load_scale_rows(nc.sync, wk_s, wk_scales[0], range(4))
+        nc.sync.dma_start(out=terr[1][:], in_=terr_rows[0, 1])
         wo_rows = wo.rearrange("(b p i) n -> b p i n", b=BLOCKS, i=PACK)
         for u in range(2):
             nc.sync.dma_start(out=terr[2 + u][:], in_=terr_rows[1, u])
@@ -181,9 +181,14 @@ def tile_list_sounding_path_features_kernel(
                 u = c // BANK
                 angle = angle_banks[u]
                 with_table(angle[:], wp_w[:, 2 * t * P : 2 * (t + 1) * P].bitcast(FP4X4), wp_s[:, cols], c)
-                level = level_banks[u]
+                level = back_banks[u] if t == 1 else level_banks[u]
                 with_table(level[:], w1_w[:, cols].bitcast(FP8X4), w1_s[:, cols], c)
-                sine = first_sine[:] if (t, u) == (0, 0) else sine_tiles[u][:]
+                if (t, u) == (0, 0):
+                    sine = first_sine[:]
+                elif t == 1:
+                    sine = picked[1][:, 3, c : c + BANK]
+                else:
+                    sine = sine_tiles[u][:]
                 nc.scalar.activation(out=sine, in_=angle[:], func=ACT.Sin, bias=phase_sb[:, b, i : i + 1])
                 if on_vector:
                     nc.vector.scalar_tensor_tensor(
@@ -232,7 +237,7 @@ def tile_list_sounding_path_features_kernel(
             with_table(acc[:], wk_w[:, cols].bitcast(FP8X4), wk_s[:, cols], c)
             nc.scalar.copy(out=skip[:, n, c : c + BANK], in_=acc[:])
 
-        late_tiles = {5: z_first[0], 6: z_first[1], 7: z_last}
+        late_tiles = {6: z_first, 7: z_last}
         gather_scales(0)
         quantise_w1(first_grouped, 0, 0, 2)
         gather_scales(1)
@@ -248,18 +253,18 @@ def tile_list_sounding_path_features_kernel(
                     put(t, h, 0, S)
                 if t == 0:
                     quantise_w1(grouped_tiles[1], 0, 2, PACK)
-                if t == 2:
-                    quantise_w1(z_first[1], 1, 0, PACK)
+                    quantise_w1(z_last, 1, 0, PACK)
                 if t < 3:
                     fetch(b, i, 0, PL)
                 if t in (4, 5):
                     quantise_wo(t - 4)
-                if t in (5, 6):
-                    weave(nc.scalar.copy, z_first[t - 5][:], 0, 0, PACK, (t - 5) * BANK, BANK)
-                    quantise_z(z_first[t - 5][:], 0, (t - 5) * BANK, BANK)
-        for n in range(NT):
-            for c in range(0, S, BANK):
-                skip_product(n, c)
+                if t == 1:
+                    for n in range(NT):
+                        for c in range(0, S, BANK):
+                            skip_product(n, c)
+                if t == 6:
+                    weave(nc.scalar.copy, z_first[:], 0, 0, PACK, 0, PL)
+                    quantise_z(z_first[:], 0, 0, PL)
         weave(nc.scalar.copy, z_last[:], 1, 0, 2, 0, PL)
 
         out_rows = out.rearrange("(n p) j -> p n j", p=P)

@@ -94,6 +94,9 @@ def tile_list_sounding_path_features_kernel(
         for page in pages:
             nc.vector.memset(page[:], 0.0)
 
+        unread = keep.tile([P, 1], F32, name="unread")
+        nc.scalar.activation(out=unread[:], in_=ident[:, 0:1], func=ACT.Silu)
+
         nc.sync.dma_start(list1[:], offs)
         load_scale_rows(nc.sync, wp_raw_s, wp_scales[0], range(0, 3))
         nc.sync.dma_start(out=tab_w[:], in_=tab_words[0].rearrange("p t i -> p (t i)").bitcast(I32))

from contextlib import ExitStack

import concourse.mybir as mybir
from concourse.masks import make_identity

K, H, N, T, S, T2, PL = 512, 1024, 384, 4096, 1024, 2048, 1024
FLOPS = 2 * (2 * K * H * S + H * N * PL + K * N * S)

F32 = mybir.dt.float32
BF16 = mybir.dt.bfloat16
I32 = mybir.dt.int32
U32 = mybir.dt.uint32
U16 = mybir.dt.uint16
U8 = mybir.dt.uint8
FP8X4 = mybir.dt.float8_e4m3fn_x4
FP4X4 = mybir.dt.float4_e2m1fn_x4
ALU = mybir.AluOpType
ACT = mybir.ActivationFunctionType

P = 128
PACK = 4
BANK = 512
BLOCKS = H // (P * PACK)
NT = N // P
CHUNKS = (256, 256, 256, 128, 128)


def load_scale_rows(queue, plane, rows, places):
    for r in places:
        queue.dma_start(out=plane[r:P:32, :].bitcast(I32), in_=rows[r:16:4, :].bitcast(I32))


def tile_list_sounding_path_features_kernel(
    tc, tab_words, tab_scales, offs, offs2, offs3, w1, wp_words, wp_scales, phase, gain, wgs, terrain, wo, wk_words, wk_scales, out
):
    nc = tc.nc
    with ExitStack() as ctx:
        keep = ctx.enter_context(tc.tile_pool(name="keep", bufs=1))
        psum = ctx.enter_context(tc.psum_pool(name="psum", bufs=1))

        def several(name, count, shape, dtype):
            return [keep.tile(shape, dtype, name="%s%d" % (name, u), align_bytes=64) for u in range(count)]

        banks = [psum.tile([P, BANK], F32, name="bank%d" % u) for u in range(8)]
        angle_banks, level_banks, turned_banks, back_banks = banks[0:2], banks[2:4], banks[4:6], banks[6:8]
        grouped_tiles = several("grouped", 2, [P, PACK * BANK], BF16)
        h_tiles = several("h", 3, [P, S], F32)
        sine_tiles = several("sine", 2, [P, BANK], F32)
        level_tiles = several("level_sb", 2, [P, BANK], F32)
        turned_tiles = several("turned_sb", 2, [P, BANK], F32)

        list1 = keep.tile([P, S // 16], U16, name="list1")
        list2 = keep.tile([P, S // 16], U16, name="list2")
        list3 = keep.tile([P, PL // 16], U16, name="list3")
        tab_w = keep.tile([P, T], I32, name="tab_w", align_bytes=64)
        tab_s = keep.tile([P, T], U8, name="tab_s", align_bytes=64)
        v_w = keep.tile([P, S], U32, name="v_w", align_bytes=64)
        shared = ctx.enter_context(tc.tile_pool(name="shared", bufs=1))
        first_grouped = shared.tile([P, 2 * BANK], BF16, name="first_grouped", align_bytes=64, offset=0)
        first_sine = shared.tile([P, BANK], F32, name="first_sine", align_bytes=64, offset=BANK)
        v_s = [
            keep.tile([P, BANK], U8, name="v_s0", align_bytes=64),
            shared.tile([P, BANK], U8, name="v_s1", align_bytes=64, offset=0),
        ]
        wp_raw_w = keep.tile([P, 2 * H], U8, name="wp_raw_w", align_bytes=64)
        wp_raw_s = keep.tile([P, H], U8, name="wp_raw_s", align_bytes=64)
        wp_w = keep.tile([P, 2 * H], U8, name="wp_w", align_bytes=64)
        wp_s = keep.tile([P, H], U8, name="wp_s", align_bytes=64)
        wk_w = keep.tile([P, N], I32, name="wk_w", align_bytes=64)
        wk_s = keep.tile([P, N], U8, name="wk_s", align_bytes=64)
        w1_raw = several("w1_raw", 2 * BLOCKS, [P, PACK, BANK // 2], F32)
        w1_w = keep.tile([P, H], U32, name="w1_w", align_bytes=64)
        w1_s = keep.tile([P, H], U8, name="w1_s", align_bytes=64)
        wo_raw = keep.tile([P, PACK, N], F32, name="wo_raw")
        ident = keep.tile([P, P], F32, name="ident")
        z_first = keep.tile([P, PACK * PL], BF16, name="z_first", align_bytes=64)
        z_last = keep.tile([P, PACK * PL], BF16, name="z_last", align_bytes=64)
        wo_w = keep.tile([P, BLOCKS * N], U32, name="wo_w", align_bytes=64)
        wo_s = keep.tile([P, BLOCKS * N], U8, name="wo_s", align_bytes=64)
        phase_sb = keep.tile([P, BLOCKS, PACK], F32, name="phase_sb")
        gain_sb = keep.tile([P, BLOCKS, PACK], F32, name="gain_sb")
        wgs_sb = keep.tile([P, S], F32, name="wgs_sb")
        terr = [keep.tile([P, 2, PL], F32, name="terr%d" % u) for u in range(2 * BLOCKS)]
        pages = [keep.tile([P, T2], F32, name="page%d" % u) for u in range(3)]
        picked = [keep.tile([P, PACK, PL], F32, name="picked%d" % b) for b in range(BLOCKS)]
        z_w = keep.tile([P, BLOCKS * PL], U32, name="z_w", align_bytes=64)
        z_s = keep.tile([P, BLOCKS * PL], U8, name="z_s", align_bytes=64)
        skip = keep.tile([P, NT, PL], F32, name="skip")

        nc.gpsimd.memset(wp_raw_s[:].bitcast(I32), 0)
        nc.gpsimd.memset(tab_s[:].bitcast(I32), 0)
        nc.gpsimd.memset(wk_s[:].bitcast(I32), 0)
        make_identity(nc, ident[:])
        for page in pages:
            nc.vector.memset(page[:], 0.0)

        unread = keep.tile([P, 1], F32, name="unread")
        nc.scalar.activation(out=unread[:], in_=ident[:, 0:1], func=ACT.Silu)

        nc.sync.dma_start(list1[:], offs)
        load_scale_rows(nc.sync, wp_raw_s, wp_scales[0], range(0, 3))
        nc.sync.dma_start(out=tab_w[:], in_=tab_words[0].rearrange("p t i -> p (t i)").bitcast(I32))
        load_scale_rows(nc.sync, wp_raw_s, wp_scales[0], range(3, 4))
        load_scale_rows(nc.sync, tab_s, tab_scales[0], range(4))
        nc.sync.dma_start(out=wp_raw_w[:].bitcast(I32), in_=wp_words[0].bitcast(I32))
        w1_rows = w1.rearrange("(p j) (u c) -> u p j c", j=PACK, u=2 * BLOCKS)
        for u in range(2):
            nc.sync.dma_start(out=w1_raw[u][:], in_=w1_rows[u])
        nc.sync.dma_start(out=phase_sb[:], in_=phase.rearrange("(b p i) -> p b i", b=BLOCKS, i=PACK))
        nc.sync.dma_start(out=gain_sb[:], in_=gain.rearrange("(b p i) -> p b i", b=BLOCKS, i=PACK))
        nc.sync.dma_start(out=wgs_sb[:], in_=wgs)
        nc.sync.dma_start(list2[:], offs2)
        nc.sync.dma_start(list3[:], offs3)
        terr_rows = terrain.rearrange("(b p u e) j -> b u p e j", b=BLOCKS, u=2, e=2)
        for u in range(2, 4):
            nc.sync.dma_start(out=w1_raw[u][:], in_=w1_rows[u])
        nc.sync.dma_start(out=terr[0][:], in_=terr_rows[0, 0])
        nc.sync.dma_start(out=wk_w[:], in_=wk_words[0].rearrange("p c i -> p (c i)").bitcast(I32))
        load_scale_rows(nc.sync, wk_s, wk_scales[0], range(4))
        nc.sync.dma_start(out=terr[1][:], in_=terr_rows[0, 1])
        wo_rows = wo.rearrange("(b p i) n -> b p i n", b=BLOCKS, i=PACK)
        for u in range(2):
            nc.sync.dma_start(out=terr[2 + u][:], in_=terr_rows[1, u])

        nc.vector.tensor_copy(
            out=wp_s[:].rearrange("p (b i m) -> p b i m", b=BLOCKS, i=PACK),
            in_=wp_raw_s[:].rearrange("p (b m i) -> p b i m", b=BLOCKS, i=PACK),
        )
        nc.scalar.copy(
            out=wp_w[:].bitcast(U16).rearrange("p (b i m) -> p b m i", b=BLOCKS, i=PACK),
            in_=wp_raw_w[:].bitcast(U16).rearrange("p (b m i) -> p b m i", b=BLOCKS, i=PACK),
        )

        def entries(lst, first, count):
            return lst[:, first // 16 : (first + count) // 16]

        for c in range(0, S, BANK):
            nc.vector.tensor_copy(v_w[:, c : c + BANK], tab_w[:].bitcast(U32).indirect(entries(list1, c, BANK)))

        def gather_scales(u):
            nc.vector.tensor_copy(v_s[u][:], tab_s[:].indirect(entries(list1, u * BANK, BANK)))

        def quantise_w1(grouped, b, i0, i1):
            width = (i1 - i0) * BANK
            for u in range(2):
                nc.scalar.copy(
                    out=grouped[:, 0:width].rearrange("p (i m j) -> p m i j", j=PACK, m=P)[:, u * P // 2 : (u + 1) * P // 2],
                    in_=w1_raw[2 * b + u][:].rearrange("p j (m i) -> p m i j", i=PACK)[:, :, i0:i1, :],
                )
            cols = slice((PACK * b + i0) * P, (PACK * b + i1) * P)
            nc.vector.quantize_mx(out=w1_w[:, cols].bitcast(FP8X4), scales=w1_s[:, cols], in_=grouped[:, 0:width])

        def quantise_wo(b):
            nc.sync.dma_start(out=wo_raw[:], in_=wo_rows[b])
            grouped = grouped_tiles[b]
            nc.scalar.copy(
                out=grouped[:, 0 : PACK * N].rearrange("p (c e i) -> p c i e", e=4, i=PACK),
                in_=wo_raw[:].rearrange("p i (c e) -> p c i e", e=4),
            )
            cols = slice(b * N, (b + 1) * N)
            nc.vector.quantize_mx(out=wo_w[:, cols].bitcast(FP8X4), scales=wo_s[:, cols], in_=grouped[:, 0 : PACK * N])

        def weave(copy, grouped, b, i0, i1, c, width):
            copy(
                out=grouped.rearrange("p (c e i) -> p c i e", e=4, i=PACK)[:, :, i0:i1, :],
                in_=picked[b][:, i0:i1, c : c + width].rearrange("p i (c e) -> p c i e", e=4),
            )

        def quantise_z(grouped, b, c, width):
            cols = slice(b * PL + c, b * PL + c + width)
            nc.vector.quantize_mx(out=z_w[:, cols].bitcast(FP8X4), scales=z_s[:, cols], in_=grouped)

        def with_table(acc, w_codes, w_scales, c):
            nc.tensor.matmul_mx(
                out=acc, lhsT=w_codes, lhsT_scale=w_scales,
                rhs=v_w[:, c : c + BANK].bitcast(FP8X4), rhs_scale=v_s[c // BANK][:], start=True, stop=True,
            )

        def features(b, i, on_vector):
            t = PACK * b + i
            cols = slice(t * P, (t + 1) * P)
            h = h_tiles[t % 3]
            for c in range(0, S, BANK):
                u = c // BANK
                angle = angle_banks[u]
                with_table(angle[:], wp_w[:, 2 * t * P : 2 * (t + 1) * P].bitcast(FP4X4), wp_s[:, cols], c)
                level = back_banks[u] if t == 1 else level_banks[u]
                with_table(level[:], w1_w[:, cols].bitcast(FP8X4), w1_s[:, cols], c)
                if (t, u) == (0, 0):
                    sine = first_sine[:]
                elif t == 1:
                    sine = picked[1][:, 3, c : c + BANK]
                else:
                    sine = sine_tiles[u][:]
                nc.scalar.activation(out=sine, in_=angle[:], func=ACT.Sin, bias=phase_sb[:, b, i : i + 1])
                if on_vector:
                    nc.vector.scalar_tensor_tensor(
                        out=h[:, c : c + BANK], in0=sine, scalar=gain_sb[:, b, i : i + 1], in1=level[:], op0=ALU.mult, op1=ALU.add
                    )
                    if t == 0:
                        put(t, h, c, BANK)
                    continue
                level_sb = picked[1][:, 2, 0:BANK] if (t, u) == (7, 1) else level_tiles[u][:]
                nc.scalar.copy(out=level_sb, in_=level[:])
                nc.scalar.activation(out=sine, in_=sine, func=ACT.Copy, scale=gain_sb[:, b, i : i + 1])
                turned = turned_banks[u]
                for q in range(0, BANK, P):
                    for term, first in ((level_sb, True), (sine, False)):
                        nc.tensor.matmul(
                            turned[:, q : q + P], lhsT=term[:, q : q + P], rhs=ident[:], is_transpose=True, start=first, stop=not first
                        )
                if c > 0 and t in late_tiles:
                    turned_sb = late_tiles[t][:].bitcast(F32)[:, 0:BANK]
                elif c == 0 and t >= 5:
                    turned_sb = picked[(t - 2) // PACK][:, (t - 2) % PACK, 0:BANK]
                else:
                    turned_sb = turned_tiles[u][:]
                nc.scalar.copy(out=turned_sb, in_=turned[:])
                back = back_banks[u]
                for q in range(0, BANK, P):
                    nc.tensor.transpose(back[:, q : q + P], turned_sb[:, q : q + P], ident[:])
                nc.scalar.copy(out=h[:, c : c + BANK], in_=back[:])
            return h

        def put(t, h, c, width):
            nc.vector.tensor_tensor(
                pages[t % 3][:].indirect(entries(list2, c, width)), h[:, c : c + width], wgs_sb[:, c : c + width], ALU.mult
            )

        def fetch(b, i, c, width):
            t = PACK * b + i
            nc.vector.tensor_tensor(
                picked[b][:, i, c : c + width], pages[t % 3][:].indirect(entries(list3, c, width)),
                terr[t // 2][:, t % 2, c : c + width], ALU.add,
            )

        def skip_product(n, c):
            acc = banks[(2 * n + c // BANK) % 4]
            cols = slice(n * P, (n + 1) * P)
            with_table(acc[:], wk_w[:, cols].bitcast(FP8X4), wk_s[:, cols], c)
            nc.scalar.copy(out=skip[:, n, c : c + BANK], in_=acc[:])

        late_tiles = {6: z_first, 7: z_last}
        gather_scales(0)
        quantise_w1(first_grouped, 0, 0, 2)
        gather_scales(1)
        for b in range(BLOCKS):
            for i in range(PACK):
                t = PACK * b + i
                h = features(b, i, t < 2)
                if t >= 5:
                    fetch((t - 2) // PACK, (t - 2) % PACK, 0, PL)
                if t == 7:
                    fetch(1, 2, 0, PL)
                if t > 0:
                    put(t, h, 0, S)
                if t == 0:
                    quantise_w1(grouped_tiles[1], 0, 2, PACK)
                    quantise_w1(z_last, 1, 0, PACK)
                if t < 3:
                    fetch(b, i, 0, PL)
                if t in (4, 5):
                    quantise_wo(t - 4)
                if t == 1:
                    for n in range(NT):
                        for c in range(0, S, BANK):
                            skip_product(n, c)
                if t == 6:
                    weave(nc.scalar.copy, z_first[:], 0, 0, PACK, 0, PL)
                    quantise_z(z_first[:], 0, 0, PL)
        weave(nc.scalar.copy, z_last[:], 1, 0, 2, 0, PL)

        out_rows = out.rearrange("(n p) j -> p n j", p=P)
        chunks = []
        free_banks = list(banks)
        first = 0
        for width in CHUNKS:
            per_bank = BANK // width
            sums = [(free_banks.pop(), n0, min(n0 + per_bank, NT)) for n0 in range(0, NT, per_bank)]
            chunks.append((first, width, sums))
            first = first + width

        def second_stage(b, c, width, sums):
            z_cols = slice(b * PL + c, b * PL + c + width)
            for acc, n0, n1 in sums:
                for n in range(n0, n1):
                    w_cols = slice(b * N + n * P, b * N + (n + 1) * P)
                    nc.tensor.matmul_mx(
                        out=acc[:, (n - n0) * width : (n - n0 + 1) * width],
                        lhsT=wo_w[:, w_cols].bitcast(FP8X4), lhsT_scale=wo_s[:, w_cols],
                        rhs=z_w[:, z_cols].bitcast(FP8X4), rhs_scale=z_s[:, z_cols],
                        start=(b == 0 and n == n0), stop=(b == BLOCKS - 1 and n == n1 - 1),
                    )

        for c, width, sums in chunks:
            second_stage(0, c, width, sums)
        for c, width, sums in chunks:
            fetch(BLOCKS - 1, PACK - 1, c, width)
        for c, width, sums in chunks:
            grouped = z_last[:, PACK * c : PACK * (c + width)]
            weave(nc.scalar.copy, grouped, 1, 2, PACK, c, width)
            quantise_z(grouped, 1, c, width)
        for k, (c, width, sums) in enumerate(chunks):
            second_stage(1, c, width, sums)
            bent = h_tiles[k % 3]
            for acc, n0, n1 in sums:
                nc.scalar.activation(out=bent[:, n0 * width : n1 * width], in_=acc[:, 0 : (n1 - n0) * width], func=ACT.Tanh)
            nc.vector.tensor_tensor(
                skip[:, :, c : c + width], bent[:, 0 : NT * width].rearrange("p (n j) -> p n j", n=NT), skip[:, :, c : c + width], ALU.add
            )
            nc.sync.dma_start(out=out_rows[:, :, c : c + width], in_=skip[:, :, c : c + width])
